import numpy as np
import ml_dtypes


def mxq(x, axis, fmt="e4m3"):
    dtype, down = {"e4m3": (ml_dtypes.float8_e4m3fn, 7), "e5m2": (ml_dtypes.float8_e5m2, 14)}[fmt]
    v = np.moveaxis(np.asarray(x, np.float32).astype(ml_dtypes.bfloat16).astype(np.float64), axis, -1)
    blocks = v.reshape(v.shape[:-1] + (-1, 32))
    amax = np.abs(blocks).max(-1, keepdims=True)
    byte = np.maximum(np.where(amax > 0, np.frexp(amax)[1] - 1 + 127, 0) - down, 1)
    scale = np.exp2(byte - 127.0)
    codes = (blocks / scale).astype(np.float32).astype(dtype).astype(np.float64)
    return np.moveaxis((codes * scale).reshape(v.shape), -1, axis)


WIDE = False


def mx_kscale(k):
    if not WIDE:
        return np.ones(k)
    levels = np.array([10, -10, 5, -5, 0])
    if k % 512:
        return np.exp2(np.random.permutation(np.resize(levels, k // 32))).repeat(32)
    a = np.empty((k // 512, 16))
    for p in range(k // 512):
        a[p, :8] = np.random.permutation(np.resize(levels, 8))
        for g in range(8):
            far = levels[np.abs(levels - a[p, g]) >= 10]
            a[p, g + 8] = far[np.random.randint(len(far))]
    return np.exp2(a.ravel()).repeat(32)


BF16 = ml_dtypes.bfloat16


def bf(x):
    return np.asarray(x, np.float32).astype(BF16)


def f64(x):
    return np.asarray(x).astype(np.float64)


E2M1 = np.array([0.0, 0.5, 1.0, 1.5, 2.0, 3.0, 4.0, 6.0, -0.0, -0.5, -1.0, -1.5, -2.0, -3.0, -4.0, -6.0])


def pack_weight(w, fmt):
    k, n = w.shape
    w = f64(bf(w)).reshape(k // 32, 32, n)
    amax = np.abs(w).max(1)
    if fmt == "e4m3":
        byte = np.frexp(amax)[1] - 1 + 127 - 7
    else:
        mant, ex = np.frexp(amax / 6.0)
        byte = np.where(mant > 0.5, ex, ex - 1) + 127
    byte = np.clip(np.where(amax > 0, byte, 1), 1, 254)
    scaled = (w * np.exp2(127.0 - byte)[:, None, :]).reshape(k, n).astype(np.float32)
    by_word = np.ascontiguousarray(scaled.reshape(k // 512, 128, 4, n).transpose(0, 1, 3, 2))
    if fmt == "e4m3":
        words = by_word.astype(ml_dtypes.float8_e4m3fn).view(np.uint8)
    else:
        c = by_word.astype(ml_dtypes.float4_e2m1fn).view(np.uint8) & 0xF
        words = c[..., 0::2] | (c[..., 1::2] << 4)
    return np.ascontiguousarray(words), np.ascontiguousarray(byte.astype(np.uint8).reshape(k // 512, 16, n))


def unpack_weight(words, scales, fmt):
    g, p, n, _ = words.shape
    if fmt == "e4m3":
        vals = np.ascontiguousarray(words).view(ml_dtypes.float8_e4m3fn).astype(np.float64)
    else:
        nib = np.empty((g, p, n, 4), np.uint8)
        nib[..., 0::2] = words & 0xF
        nib[..., 1::2] = words >> 4
        vals = E2M1[nib]
    vals = vals * np.repeat(np.exp2(scales.astype(np.float64) - 127.0), 8, axis=1)[..., None]
    return vals.transpose(0, 1, 3, 2).reshape(g * 512, n)
def pack4(w):
    words, scales = pack_weight(w, "e2m1")
    return words.reshape(words.shape[0], 128, -1), scales


def unpack4(words, scales):
    return unpack_weight(words.reshape(words.shape[0], 128, -1, 2), scales, "e2m1")


def planes(Y):
    n, m = Y.shape
    b = f64(bf(Y)).reshape(n // 32, 32, m)
    amax = np.abs(b).max(1)
    byte = np.clip(np.where(amax > 0, np.frexp(amax)[1] - 1 + 127 - 7, 1), 1, 254)
    codes = (b * np.exp2(127.0 - byte)[:, None, :]).reshape(n, m).astype(np.float32).astype(ml_dtypes.float8_e4m3fn).view(np.uint8)
    words = codes.reshape(n // 512, 128, 4, m).transpose(0, 1, 3, 2)
    return np.ascontiguousarray(words), np.ascontiguousarray(byte.astype(np.uint8).reshape(n // 512, 16, m))


M, K, F, N = 2048, 512, 1024, 1536


def setup_inputs():
    s = mx_kscale(K)
    t = mx_kscale(F)
    u = np.random.uniform(-1.0, 1.0, (M, 1))
    v = np.random.uniform(-1.0, 1.0, (M, 1))
    fu = np.random.randn(1, K // 2)
    fv = np.random.randn(1, K // 2)
    angle = 3.0 * np.pi * (u * fu + v * fv)
    code = np.concatenate([np.cos(angle), np.sin(angle)], axis=1)
    w1 = 0.7 * np.random.randn(K, F) / np.sqrt(K)
    w2 = np.random.randn(F, N) / np.sqrt(F)
    w1_words, w1_scales = pack4(w1 / s[:, None])
    w2_words, w2_scales = pack4(w2 / t[:, None])
    return {
        "x": bf(code * s[None, :]),
        "w1_words": w1_words,
        "w1_scales": w1_scales,
        "a1": bf((1.0 + 0.1 * np.random.randn(F)) * t),
        "w2_words": w2_words,
        "w2_scales": w2_scales,
        "b2": bf(0.25 * np.random.randn(N)),
        "a2": bf(np.exp(0.8 * np.random.randn(N))),
    }

def reference(x, w1_words, w1_scales, a1, w2_words, w2_scales, b2, a2):
    W1 = unpack4(w1_words, w1_scales)
    W2 = unpack4(w2_words, w2_scales)
    z1 = mxq(f64(x), 1, "e4m3") @ W1
    h = np.sin(z1) * f64(a1)
    z2 = mxq(h, 1, "e4m3") @ W2
    y = np.sin(z2 + f64(b2)) * f64(a2)
    Y = y.T
    words, scales = planes(Y)
    return y, words, scales

@@ -1,0 +1,362 @@
+import math
+from contextlib import ExitStack
+
+import concourse.mybir as mybir
+from concourse.masks import make_identity
+
+M, K, F, N = 2048, 512, 1024, 1536
+FLOPS = 2 * M * K * F + 2 * M * F * N
+
+F32 = mybir.dt.float32
+BF16 = mybir.dt.bfloat16
+I32 = mybir.dt.int32
+U32 = mybir.dt.uint32
+U8 = mybir.dt.uint8
+FP8X4 = mybir.dt.float8_e4m3fn_x4
+FP4X4 = mybir.dt.float4_e2m1fn_x4
+ALU = mybir.AluOpType
+ACT = mybir.ActivationFunctionType
+
+P = 128
+PASS = 512
+CHUNK = 512
+HALF = 256
+CHUNKS = M // CHUNK
+TURN = 2.0 * math.pi
+ROUNDER = 1.5 * 2.0**23
+SCALAR_ROUNDS_EVERY = 4
+TAIL = 0
+
+
+def step_order():
+    first = [("first", c, g, h) for c in range(CHUNKS) for h in range(2) for g in range(F // PASS)]
+    second = [("second", c, g, h) for c in range(CHUNKS) for g in range(N // PASS) for h in range(2)]
+    order = first[:8]
+    for i, item in enumerate(first[8:]):
+        order = order + [item] + second[2 * i : 2 * i + 2]
+    return order + second[2 * len(first[8:]) :]
+
+
+def tile_fourier_sine_field_planes_h1_kernel(
+    tc, x, w1_words, w1_scales, a1, w2_words, w2_scales, b2, a2, out_0, out_1, out_2
+):
+    nc = tc.nc
+    with ExitStack() as ctx:
+        keep = ctx.enter_context(tc.tile_pool(name="keep", bufs=1))
+        work = ctx.enter_context(tc.tile_pool(name="work", bufs=3))
+        psum = ctx.enter_context(tc.psum_pool(name="psum", bufs=8))
+        ctx.enter_context(tc.manual_schedule())
+
+        def bank(shape):
+            return psum.tile(shape, F32, name="bank")
+
+        ident = keep.tile([P, P], F32, name="ident")
+        make_identity(nc, ident[:])
+        w1_plane_in = keep.tile([P, F], U8, name="w1_plane_in", align_bytes=64)
+        nc.vector.memset(w1_plane_in[:].bitcast(I32), 0)
+        b2_rows = keep.tile([P, P], BF16, name="b2_rows")
+        nc.vector.memset(b2_rows[:], 0.0)
+        w2_plane = keep.tile([P, 2, N], U8, name="w2_plane", align_bytes=64)
+        nc.gpsimd.memset(w2_plane[:].rearrange("p g n -> p (g n)").bitcast(I32), 0)
+        warm_in = keep.tile([P, 1], F32, name="warm_in")
+        nc.vector.memset(warm_in[:], 0.0)
+        warm_out = keep.tile([P, 1], F32, name="warm_out")
+        nc.scalar.activation(out=warm_out[:], in_=warm_in[:], func=ACT.Sin)
+
+        x_in = {}
+
+        def load_x(c, h):
+            x_half = keep.tile([P, 2, K], BF16, name="x_%d_%d" % (c, h))
+            rows = x[c * CHUNK + h * HALF : c * CHUNK + (h + 1) * HALF, :]
+            nc.sync.dma_start(out=x_half[:], in_=rows.rearrange("(j p) k -> p j k", p=P))
+            x_in[c, h] = x_half
+
+        load_x(0, 0)
+        w1_in = keep.tile([P, 2 * F], U8, name="w1_in", align_bytes=64)
+        nc.sync.dma_start(out=w1_in[:].bitcast(I32), in_=w1_words[0].bitcast(I32))
+        for q in range(4):
+            nc.sync.dma_start(
+                out=w1_plane_in[32 * q : 32 * q + 4, :].bitcast(I32),
+                in_=w1_scales[0, 4 * q : 4 * q + 4, :].bitcast(I32),
+            )
+        load_x(0, 1)
+        a1_sb = keep.tile([P, F // PASS, 4], BF16, name="a1_sb")
+        nc.sync.dma_start(out=a1_sb[:], in_=a1.rearrange("(g p t) -> p g t", p=P, t=4))
+        load_x(1, 0)
+        load_x(1, 1)
+        nc.sync.dma_start(out=b2_rows[0 : N // P, :], in_=b2.rearrange("(f p) -> f p", p=P))
+        w2 = keep.tile([P, 2, 2 * N], U8, name="w2", align_bytes=64)
+        nc.sync.dma_start(out=w2[:].bitcast(I32), in_=w2_words.rearrange("g p b -> p g b").bitcast(I32))
+        for q in range(4):
+            nc.sync.dma_start(
+                out=w2_plane[32 * q : 32 * q + 4, :, :].bitcast(I32),
+                in_=w2_scales[:, 4 * q : 4 * q + 4, :].rearrange("g r n -> r g n").bitcast(I32),
+            )
+        a2_sb = keep.tile([P, N], BF16, name="a2_sb")
+        nc.sync.dma_start(out=a2_sb[:], in_=a2.partition_broadcast(P))
+        for c in range(2, CHUNKS):
+            for h in range(2):
+                load_x(c, h)
+
+        w1 = {}
+
+        def sort_w1(g):
+            codes = keep.tile([P, 2 * PASS], U8, name="w1_codes_%d" % g, align_bytes=64)
+            plane = keep.tile([P, PASS], U8, name="w1_plane_%d" % g, align_bytes=64)
+            nc.vector.tensor_copy(
+                out=codes[:].rearrange("p (t m b) -> p t m b", t=4, b=2),
+                in_=w1_in[:, g * 2 * PASS : (g + 1) * 2 * PASS].rearrange("p (m t b) -> p t m b", t=4, b=2),
+            )
+            nc.vector.tensor_copy(
+                out=plane[:].rearrange("p (t m) -> p t m", t=4),
+                in_=w1_plane_in[:, g * PASS : (g + 1) * PASS].rearrange("p (m t) -> p t m", t=4),
+            )
+            w1[g] = (codes, plane)
+
+        b2_turns = keep.tile([P, N // P], F32, name="b2_turns")
+
+        def spread_b2():
+            b2_wide = keep.tile([P, P], F32, name="b2_wide")
+            nc.vector.tensor_scalar(out=b2_wide[:], in0=b2_rows[:], scalar1=1.0 / TURN, scalar2=None, op0=ALU.mult)
+            turned = bank([P, P])
+            nc.tensor.transpose(turned[:], b2_wide[:], ident[:])
+            nc.scalar.copy(out=b2_turns[:], in_=turned[:, 0 : N // P])
+
+        def turn_words(word_blocks, name):
+            turned = bank([P, 2, 2, P])
+            for j in range(2):
+                for u in range(2):
+                    nc.tensor.transpose(turned[:, j, u, :], word_blocks(j, u), ident[:])
+            grouped = work.tile([P, 4 * HALF], BF16, name=name, align_bytes=64)
+            nc.scalar.copy(
+                out=grouped[:].bitcast(F32).rearrange("p (j r u) -> p j r u", j=2, u=2),
+                in_=turned[:].rearrange("p j u r -> p j r u"),
+            )
+            return grouped
+
+        x_grouped, x_q = {}, {}
+
+        def turn_x(c, h):
+            words = x_in[c, h][:].rearrange("p j k -> p (j k)").bitcast(F32)
+            x_grouped[c, h] = turn_words(lambda j, u: words[:, 256 * j + u : 256 * (j + 1) : 2], "x_grouped")
+
+        def quantize_x(c, h):
+            codes = work.tile([P, HALF], U32, name="x_codes", align_bytes=64)
+            plane = work.tile([P, HALF], U8, name="x_plane", align_bytes=64)
+            nc.vector.quantize_mx(out=codes[:].bitcast(FP8X4), scales=plane[:], in_=x_grouped[c, h][:])
+            x_q[c, h] = (codes, plane)
+
+        h_q = {}
+        for c in range(CHUNKS):
+            for g in range(F // PASS):
+                h_codes = keep.tile([P, CHUNK], U32, name="h_codes_%d_%d" % (c, g), align_bytes=64)
+                h_plane = keep.tile([P, CHUNK], U8, name="h_plane_%d_%d" % (c, g), align_bytes=64)
+                h_q[c, g] = (h_codes, h_plane)
+        y_planes = {}
+        for c in range(CHUNKS):
+            y_plane = keep.tile([P, CHUNK], U8, name="y_plane_%d" % c, align_bytes=64)
+            y_planes[c] = y_plane
+
+        turns, counts, rest, sines, rounded, results, y_grouped = {}, {}, {}, {}, {}, {}, {}
+
+        def multiply(item):
+            kind, c, g, h = item
+            angle = work.tile([P, 2, PASS], F32, name="angle", bufs=6)
+            for j in range(2):
+                if kind == "first":
+                    z = bank([P, 4, P])
+                    codes, plane = x_q[c, h]
+                    for t in range(4):
+                        nc.tensor.matmul_mx(
+                            out=z[:, t, :],
+                            lhsT=w1[g][0][:, 2 * P * t : 2 * P * (t + 1)].bitcast(FP4X4),
+                            lhsT_scale=w1[g][1][:, P * t : P * (t + 1)],
+                            rhs=codes[:, P * j : P * (j + 1)].bitcast(FP8X4),
+                            rhs_scale=plane[:, P * j : P * (j + 1)],
+                            start=True,
+                            stop=True,
+                        )
+                    nc.scalar.activation(
+                        out=angle[:, j, :].rearrange("p (n t) -> p n t", t=4),
+                        in_=z[:].rearrange("p t n -> p n t"),
+                        func=ACT.Copy,
+                        scale=1.0 / TURN,
+                    )
+                else:
+                    z = bank([P, CHUNK])
+                    block = 4 * g + 2 * h + j
+                    for k in range(F // PASS):
+                        nc.tensor.matmul_mx(
+                            out=z[:],
+                            lhsT=w2[:, k, 2 * P * block : 2 * P * (block + 1)].bitcast(FP4X4),
+                            lhsT_scale=w2_plane[:, k, P * block : P * (block + 1)],
+                            rhs=h_q[c, k][0][:].bitcast(FP8X4),
+                            rhs_scale=h_q[c, k][1][:],
+                            start=(k == 0),
+                            stop=(k == F // PASS - 1),
+                        )
+                    nc.scalar.activation(
+                        out=angle[:, j, :],
+                        in_=z[:],
+                        func=ACT.Identity,
+                        scale=1.0 / TURN,
+                        bias=b2_turns[:, block : block + 1],
+                    )
+            turns[item] = angle
+
+        def count_on_scalar(item):
+            count = work.tile([P, 2, PASS], U32, name="count")
+            nc.scalar.activation(out=count[:], in_=turns[item][:], func=ACT.Copy, bias=ROUNDER)
+            counts[item] = count[:].bitcast(I32)
+
+        def count_on_vector(item):
+            count = work.tile([P, 2, PASS], I32, name="count")
+            nc.vector.tensor_scalar(out=count[:], in0=turns[item][:], scalar1=ROUNDER, scalar2=None, op0=ALU.add)
+            counts[item] = count[:]
+
+        def reduce_angle(item):
+            part = work.tile([P, 2, PASS], F32, name="part", bufs=5)
+            if item[0] == "first":
+                nc.vector.scalar_tensor_tensor(
+                    out=part[:], in0=counts[item], scalar=ROUNDER, in1=turns[item][:],
+                    op0=ALU.subtract, op1=ALU.subtract,
+                )
+            else:
+                nc.vector.tensor_scalar(
+                    out=part[:], in0=counts[item], scalar1=ROUNDER, scalar2=-1.0, op0=ALU.subtract, op1=ALU.mult
+                )
+            rest[item] = part
+
+        def sine(item):
+            kind, c, g, h = item
+            s = work.tile([P, 2, PASS], F32, name="sine")
+            if kind == "first":
+                nc.scalar.activation(out=s[:], in_=rest[item][:], func=ACT.Sin, scale=-TURN)
+            else:
+                for j in range(2):
+                    frac = bank([P, 4, P])
+                    tokens = slice((2 * h + j) * P, (2 * h + j + 1) * P)
+                    for b in range(4):
+                        source = (kind, c, g, b // 2)
+                        nc.tensor.matmul(
+                            frac[:, b, :], lhsT=rest[source][:, b % 2, tokens], rhs=ident[:],
+                            is_transpose=True, start=True, stop=False,
+                        )
+                        nc.tensor.matmul(
+                            frac[:, b, :], lhsT=turns[source][:, b % 2, tokens], rhs=ident[:],
+                            is_transpose=True, start=False, stop=True,
+                        )
+                    nc.scalar.activation(
+                        out=s[:, j, :], in_=frac[:].rearrange("p b f -> p (b f)"), func=ACT.Sin, scale=TURN
+                    )
+            sines[item] = s
+
+        def amplify(item):
+            kind, c, g, h = item
+            if kind == "first":
+                hb = work.tile([P, 4 * HALF], BF16, name="h_grouped", align_bytes=64)
+                nc.vector.tensor_tensor(
+                    out=hb[:].rearrange("p (n t) -> p n t", t=4),
+                    in0=sines[item][:].rearrange("p j (n t) -> p (j n) t", t=4),
+                    in1=a1_sb[:, g, :].unsqueeze(1).to_broadcast([P, HALF, 4]),
+                    op=ALU.mult,
+                )
+                rounded[item] = hb
+            else:
+                y = work.tile([P, 2, PASS], F32, name="y", bufs=4)
+                nc.vector.tensor_tensor(
+                    out=y[:],
+                    in0=sines[item][:],
+                    in1=a2_sb[:, g * PASS : (g + 1) * PASS].unsqueeze(1).to_broadcast([P, 2, PASS]),
+                    op=ALU.mult,
+                )
+                rows = out_0[c * CHUNK + h * HALF : c * CHUNK + (h + 1) * HALF, g * PASS : (g + 1) * PASS]
+                nc.sync.dma_start(out=rows.rearrange("(j p) n -> p j n", p=P), in_=y[:])
+                results[item] = y
+
+        def round_y(item, copy):
+            yb = work.tile([P, 2, 2, P, 2], BF16, name="y_sorted")
+            copy(out=yb[:], in_=results[item][:].rearrange("p j (m u e) -> p j u m e", u=2, e=2))
+            rounded[item] = yb
+
+        def turn_y(item):
+            words = rounded[item][:].rearrange("p j u m e -> p (j u m e)").bitcast(F32)
+            y_grouped[item] = turn_words(lambda j, u: words[:, (2 * j + u) * P : (2 * j + u + 1) * P], "y_grouped")
+
+        def quantize_h(item):
+            kind, c, g, h = item
+            cols = slice(h * HALF, (h + 1) * HALF)
+            nc.vector.quantize_mx(
+                out=h_q[c, g][0][:, cols].bitcast(FP8X4), scales=h_q[c, g][1][:, cols], in_=rounded[item][:]
+            )
+
+        def quantize_y(item):
+            kind, c, g, h = item
+            cols = slice(h * HALF, (h + 1) * HALF)
+            codes = work.tile([P, HALF], U32, name="y_codes", align_bytes=64)
+            nc.vector.quantize_mx(
+                out=codes[:].bitcast(FP8X4), scales=y_planes[c][4 * g : P, cols], in_=y_grouped[item][:]
+            )
+            tokens = slice(c * CHUNK + h * HALF, c * CHUNK + (h + 1) * HALF)
+            nc.sync.dma_start(
+                out=out_1[g, :, tokens, :].rearrange("p m t -> p (m t)").bitcast(I32), in_=codes[:].bitcast(I32)
+            )
+            if (g, h) == (N // PASS - 1, 1):
+                for q in range(4):
+                    nc.sync.dma_start(
+                        out=out_2[:, 4 * q : 4 * q + 4, c * CHUNK : (c + 1) * CHUNK].bitcast(I32),
+                        in_=y_planes[c][32 * q : 32 * q + 12, :].bitcast(I32),
+                    )
+
+        order = step_order()
+
+        def at(n, kind=None):
+            if 0 <= n < len(order) and kind in (None, order[n][0]):
+                return [order[n]]
+            return []
+
+        def x_for(n):
+            return [(c, h) for (kind, c, g, h) in at(n, "first") if g == 0]
+
+        sort_w1(0)
+        turn_x(0, 0)
+        quantize_x(0, 0)
+        sort_w1(1)
+        turn_x(0, 1)
+        steps = len(order)
+
+        def on_scalar(i):
+            return i % SCALAR_ROUNDS_EVERY == 2 and i < steps - TAIL
+
+        for n in range(steps + 7):
+            for item in at(n):
+                multiply(item)
+            for item in at(n - 1):
+                if not on_scalar(n - 1):
+                    count_on_vector(item)
+            for item in at(n - 3):
+                sine(item)
+            for item in at(n - 4):
+                amplify(item)
+            for item in at(n - 1):
+                reduce_angle(item)
+            for item in at(n):
+                if on_scalar(n):
+                    count_on_scalar(item)
+            for item in at(n - 5, "second"):
+                if n - 5 >= steps - TAIL:
+                    round_y(item, nc.scalar.copy)
+                turn_y(item)
+            for c, h in x_for(n + 3):
+                turn_x(c, h)
+            for item in at(n - 4, "second"):
+                if n - 4 < steps - TAIL:
+                    round_y(item, nc.vector.tensor_copy)
+            for item in at(n - 4, "first"):
+                quantize_h(item)
+            for c, h in x_for(n + 2):
+                quantize_x(c, h)
+            for item in at(n - 6, "second"):
+                quantize_y(item)
+            if n == 4:
+                spread_b2()

@@ -24,17 +24,23 @@ HALF = 256
 CHUNKS = M // CHUNK
 TURN = 2.0 * math.pi
 ROUNDER = 1.5 * 2.0**23
-SCALAR_ROUNDS_EVERY = 4
+SCALAR_ROUNDS_EVERY = 8
 TAIL = 0
+LAST = 1
+FROM = 0
+HEAD = 8
+XV = 1
+PH = 6
+DA = 3
 
 
 def step_order():
     first = [("first", c, g, h) for c in range(CHUNKS) for h in range(2) for g in range(F // PASS)]
     second = [("second", c, g, h) for c in range(CHUNKS) for g in range(N // PASS) for h in range(2)]
-    order = first[:8]
-    for i, item in enumerate(first[8:]):
-        order = order + [item] + second[2 * i : 2 * i + 2]
-    return order + second[2 * len(first[8:]) :]
+    order = first[:HEAD]
+    for i in range(HEAD, len(first), 2):
+        order = order + second[i - HEAD : i - HEAD + 2] + first[i : i + 2]
+    return order + second[len(first) - HEAD :]
 
 
 def tile_fourier_sine_field_planes_h1_kernel(
@@ -52,8 +58,8 @@ def tile_fourier_sine_field_planes_h1_kernel(
 
         ident = keep.tile([P, P], F32, name="ident")
         make_identity(nc, ident[:])
-        w1_plane_in = keep.tile([P, F], U8, name="w1_plane_in", align_bytes=64)
-        nc.vector.memset(w1_plane_in[:].bitcast(I32), 0)
+        w1_plane = keep.tile([P, F], U8, name="w1_plane", align_bytes=64)
+        nc.vector.memset(w1_plane[:].bitcast(I32), 0)
         b2_rows = keep.tile([P, P], BF16, name="b2_rows")
         nc.vector.memset(b2_rows[:], 0.0)
         w2_plane = keep.tile([P, 2, N], U8, name="w2_plane", align_bytes=64)
@@ -72,11 +78,11 @@ def tile_fourier_sine_field_planes_h1_kernel(
             x_in[c, h] = x_half
 
         load_x(0, 0)
-        w1_in = keep.tile([P, 2 * F], U8, name="w1_in", align_bytes=64)
-        nc.sync.dma_start(out=w1_in[:].bitcast(I32), in_=w1_words[0].bitcast(I32))
+        w1 = keep.tile([P, 2 * F], U8, name="w1", align_bytes=64)
+        nc.sync.dma_start(out=w1[:].bitcast(I32), in_=w1_words[0].bitcast(I32))
         for q in range(4):
             nc.sync.dma_start(
-                out=w1_plane_in[32 * q : 32 * q + 4, :].bitcast(I32),
+                out=w1_plane[32 * q : 32 * q + 4, :].bitcast(I32),
                 in_=w1_scales[0, 4 * q : 4 * q + 4, :].bitcast(I32),
             )
         load_x(0, 1)
@@ -98,37 +104,25 @@ def tile_fourier_sine_field_planes_h1_kernel(
             for h in range(2):
                 load_x(c, h)
 
-        w1 = {}
-
-        def sort_w1(g):
-            codes = keep.tile([P, 2 * PASS], U8, name="w1_codes_%d" % g, align_bytes=64)
-            plane = keep.tile([P, PASS], U8, name="w1_plane_%d" % g, align_bytes=64)
-            nc.vector.tensor_copy(
-                out=codes[:].rearrange("p (t m b) -> p t m b", t=4, b=2),
-                in_=w1_in[:, g * 2 * PASS : (g + 1) * 2 * PASS].rearrange("p (m t b) -> p t m b", t=4, b=2),
-            )
-            nc.vector.tensor_copy(
-                out=plane[:].rearrange("p (t m) -> p t m", t=4),
-                in_=w1_plane_in[:, g * PASS : (g + 1) * PASS].rearrange("p (m t) -> p t m", t=4),
-            )
-            w1[g] = (codes, plane)
-
         b2_turns = keep.tile([P, N // P], F32, name="b2_turns")
 
-        def spread_b2():
-            b2_wide = keep.tile([P, P], F32, name="b2_wide")
+        b2_wide = keep.tile([P, P], F32, name="b2_wide")
+
+        def scale_b2():
             nc.vector.tensor_scalar(out=b2_wide[:], in0=b2_rows[:], scalar1=1.0 / TURN, scalar2=None, op0=ALU.mult)
+
+        def spread_b2():
             turned = bank([P, P])
             nc.tensor.transpose(turned[:], b2_wide[:], ident[:])
             nc.scalar.copy(out=b2_turns[:], in_=turned[:, 0 : N // P])
 
-        def turn_words(word_blocks, name):
+        def turn_words(word_blocks, name, copy):
             turned = bank([P, 2, 2, P])
             for j in range(2):
                 for u in range(2):
                     nc.tensor.transpose(turned[:, j, u, :], word_blocks(j, u), ident[:])
             grouped = work.tile([P, 4 * HALF], BF16, name=name, align_bytes=64)
-            nc.scalar.copy(
+            copy(
                 out=grouped[:].bitcast(F32).rearrange("p (j r u) -> p j r u", j=2, u=2),
                 in_=turned[:].rearrange("p j u r -> p j r u"),
             )
@@ -136,9 +130,9 @@ def tile_fourier_sine_field_planes_h1_kernel(
 
         x_grouped, x_q = {}, {}
 
-        def turn_x(c, h):
+        def turn_x(c, h, copy):
             words = x_in[c, h][:].rearrange("p j k -> p (j k)").bitcast(F32)
-            x_grouped[c, h] = turn_words(lambda j, u: words[:, 256 * j + u : 256 * (j + 1) : 2], "x_grouped")
+            x_grouped[c, h] = turn_words(lambda j, u: words[:, 256 * j + u : 256 * (j + 1) : 2], "x_grouped", copy)
 
         def quantize_x(c, h):
             codes = work.tile([P, HALF], U32, name="x_codes", align_bytes=64)
@@ -164,21 +158,20 @@ def tile_fourier_sine_field_planes_h1_kernel(
             angle = work.tile([P, 2, PASS], F32, name="angle", bufs=6)
             for j in range(2):
                 if kind == "first":
-                    z = bank([P, 4, P])
+                    z = bank([P, PASS])
                     codes, plane = x_q[c, h]
-                    for t in range(4):
-                        nc.tensor.matmul_mx(
-                            out=z[:, t, :],
-                            lhsT=w1[g][0][:, 2 * P * t : 2 * P * (t + 1)].bitcast(FP4X4),
-                            lhsT_scale=w1[g][1][:, P * t : P * (t + 1)],
-                            rhs=codes[:, P * j : P * (j + 1)].bitcast(FP8X4),
-                            rhs_scale=plane[:, P * j : P * (j + 1)],
-                            start=True,
-                            stop=True,
-                        )
+                    nc.tensor.matmul_mx(
+                        out=z[:],
+                        lhsT=codes[:, P * j : P * (j + 1)].bitcast(FP8X4),
+                        lhsT_scale=plane[:, P * j : P * (j + 1)],
+                        rhs=w1[:, 2 * PASS * g : 2 * PASS * (g + 1)].bitcast(FP4X4),
+                        rhs_scale=w1_plane[:, PASS * g : PASS * (g + 1)],
+                        start=True,
+                        stop=True,
+                    )
                     nc.scalar.activation(
-                        out=angle[:, j, :].rearrange("p (n t) -> p n t", t=4),
-                        in_=z[:].rearrange("p t n -> p n t"),
+                        out=angle[:, j, :].rearrange("p (t m) -> p t m", t=4),
+                        in_=z[:].rearrange("p (m t) -> p t m", t=4),
                         func=ACT.Copy,
                         scale=1.0 / TURN,
                     )
@@ -216,36 +209,35 @@ def tile_fourier_sine_field_planes_h1_kernel(
 
         def reduce_angle(item):
             part = work.tile([P, 2, PASS], F32, name="part", bufs=5)
-            if item[0] == "first":
-                nc.vector.scalar_tensor_tensor(
-                    out=part[:], in0=counts[item], scalar=ROUNDER, in1=turns[item][:],
-                    op0=ALU.subtract, op1=ALU.subtract,
-                )
-            else:
-                nc.vector.tensor_scalar(
-                    out=part[:], in0=counts[item], scalar1=ROUNDER, scalar2=-1.0, op0=ALU.subtract, op1=ALU.mult
-                )
+            nc.vector.tensor_scalar(
+                out=part[:], in0=counts[item], scalar1=ROUNDER, scalar2=-1.0, op0=ALU.subtract, op1=ALU.mult
+            )
             rest[item] = part
 
         def sine(item):
             kind, c, g, h = item
             s = work.tile([P, 2, PASS], F32, name="sine")
-            if kind == "first":
-                nc.scalar.activation(out=s[:], in_=rest[item][:], func=ACT.Sin, scale=-TURN)
-            else:
-                for j in range(2):
-                    frac = bank([P, 4, P])
-                    tokens = slice((2 * h + j) * P, (2 * h + j + 1) * P)
-                    for b in range(4):
-                        source = (kind, c, g, b // 2)
-                        nc.tensor.matmul(
-                            frac[:, b, :], lhsT=rest[source][:, b % 2, tokens], rhs=ident[:],
-                            is_transpose=True, start=True, stop=False,
-                        )
-                        nc.tensor.matmul(
-                            frac[:, b, :], lhsT=turns[source][:, b % 2, tokens], rhs=ident[:],
-                            is_transpose=True, start=False, stop=True,
-                        )
+            for j in range(2):
+                frac = bank([P, 4, P])
+                for b in range(4):
+                    if kind == "first":
+                        source, row, cols = item, j, slice(b * P, (b + 1) * P)
+                    else:
+                        source, row, cols = (kind, c, g, b // 2), b % 2, slice((2 * h + j) * P, (2 * h + j + 1) * P)
+                    nc.tensor.matmul(
+                        frac[:, b, :], lhsT=rest[source][:, row, cols], rhs=ident[:],
+                        is_transpose=True, start=True, stop=False,
+                    )
+                    nc.tensor.matmul(
+                        frac[:, b, :], lhsT=turns[source][:, row, cols], rhs=ident[:],
+                        is_transpose=True, start=False, stop=True,
+                    )
+                if kind == "first":
+                    nc.scalar.activation(
+                        out=s[:, j, :].rearrange("p (n t) -> p n t", t=4),
+                        in_=frac[:].rearrange("p t n -> p n t"), func=ACT.Sin, scale=TURN
+                    )
+                else:
                     nc.scalar.activation(
                         out=s[:, j, :], in_=frac[:].rearrange("p b f -> p (b f)"), func=ACT.Sin, scale=TURN
                     )
@@ -281,7 +273,7 @@ def tile_fourier_sine_field_planes_h1_kernel(
 
         def turn_y(item):
             words = rounded[item][:].rearrange("p j u m e -> p (j u m e)").bitcast(F32)
-            y_grouped[item] = turn_words(lambda j, u: words[:, (2 * j + u) * P : (2 * j + u + 1) * P], "y_grouped")
+            y_grouped[item] = turn_words(lambda j, u: words[:, (2 * j + u) * P : (2 * j + u + 1) * P], "y_grouped", nc.scalar.copy)
 
         def quantize_h(item):
             kind, c, g, h = item
@@ -318,15 +310,13 @@ def tile_fourier_sine_field_planes_h1_kernel(
         def x_for(n):
             return [(c, h) for (kind, c, g, h) in at(n, "first") if g == 0]
 
-        sort_w1(0)
-        turn_x(0, 0)
+        turn_x(0, 0, nc.vector.tensor_copy)
         quantize_x(0, 0)
-        sort_w1(1)
-        turn_x(0, 1)
+        turn_x(0, 1, nc.vector.tensor_copy)
         steps = len(order)
 
         def on_scalar(i):
-            return i % SCALAR_ROUNDS_EVERY == 2 and i < steps - TAIL
+            return i % SCALAR_ROUNDS_EVERY == PH and i >= FROM
 
         for n in range(steps + 7):
             for item in at(n):
@@ -334,9 +324,9 @@ def tile_fourier_sine_field_planes_h1_kernel(
             for item in at(n - 1):
                 if not on_scalar(n - 1):
                     count_on_vector(item)
-            for item in at(n - 3):
+            for item in at(n - DA, "first") + at(n - 3, "second"):
                 sine(item)
-            for item in at(n - 4):
+            for item in at(n - DA - 1, "first") + at(n - 4, "second"):
                 amplify(item)
             for item in at(n - 1):
                 reduce_angle(item)
@@ -344,19 +334,21 @@ def tile_fourier_sine_field_planes_h1_kernel(
                 if on_scalar(n):
                     count_on_scalar(item)
             for item in at(n - 5, "second"):
-                if n - 5 >= steps - TAIL:
+                if steps - TAIL <= n - 5 < steps - LAST:
                     round_y(item, nc.scalar.copy)
                 turn_y(item)
             for c, h in x_for(n + 3):
-                turn_x(c, h)
+                turn_x(c, h, nc.vector.tensor_copy if c < XV else nc.scalar.copy)
             for item in at(n - 4, "second"):
-                if n - 4 < steps - TAIL:
+                if not steps - TAIL <= n - 4 < steps - LAST:
                     round_y(item, nc.vector.tensor_copy)
-            for item in at(n - 4, "first"):
+            for item in at(n - DA - 1, "first"):
                 quantize_h(item)
             for c, h in x_for(n + 2):
                 quantize_x(c, h)
             for item in at(n - 6, "second"):
                 quantize_y(item)
+            if n == 2:
+                scale_b2()
             if n == 4:
                 spread_b2()

@@ -25,8 +25,9 @@ CHUNKS = M // CHUNK
 TURN = 2.0 * math.pi
 ROUNDER = 1.5 * 2.0**23
 SCALAR_ROUNDS_EVERY = 8
-TAIL = 0
-LAST = 1
+TAIL = 4
+SHARED = 1
+LAST = 2
 FROM = 0
 HEAD = 8
 XV = 1
@@ -148,8 +149,9 @@ def tile_fourier_sine_field_planes_h1_kernel(
                 h_q[c, g] = (h_codes, h_plane)
         y_planes = {}
         for c in range(CHUNKS):
-            y_plane = keep.tile([P, CHUNK], U8, name="y_plane_%d" % c, align_bytes=64)
-            y_planes[c] = y_plane
+            for pair in range(2):
+                y_plane = keep.tile([P, CHUNK], U8, name="y_plane_%d_%d" % (c, pair), align_bytes=64)
+                y_planes[c, pair] = y_plane
 
         turns, counts, rest, sines, rounded, results, y_grouped = {}, {}, {}, {}, {}, {}, {}
 
@@ -169,12 +171,14 @@ def tile_fourier_sine_field_planes_h1_kernel(
                         start=True,
                         stop=True,
                     )
-                    nc.scalar.activation(
-                        out=angle[:, j, :].rearrange("p (t m) -> p t m", t=4),
-                        in_=z[:].rearrange("p (m t) -> p t m", t=4),
-                        func=ACT.Copy,
-                        scale=1.0 / TURN,
-                    )
+                    sorted_out = angle[:, j, :].rearrange("p (t m) -> p t m", t=4)
+                    sorted_in = z[:].rearrange("p (m t) -> p t m", t=4)
+                    if j == 1 and item in order[:SHARED]:
+                        nc.vector.tensor_scalar(
+                            out=sorted_out, in0=sorted_in, scalar1=1.0 / TURN, scalar2=None, op0=ALU.mult
+                        )
+                    else:
+                        nc.scalar.activation(out=sorted_out, in_=sorted_in, func=ACT.Copy, scale=1.0 / TURN)
                 else:
                     z = bank([P, CHUNK])
                     block = 4 * g + 2 * h + j
@@ -287,17 +291,20 @@ def tile_fourier_sine_field_planes_h1_kernel(
             cols = slice(h * HALF, (h + 1) * HALF)
             codes = work.tile([P, HALF], U32, name="y_codes", align_bytes=64)
             nc.vector.quantize_mx(
-                out=codes[:].bitcast(FP8X4), scales=y_planes[c][4 * g : P, cols], in_=y_grouped[item][:]
+                out=codes[:].bitcast(FP8X4), scales=y_planes[c, min(g, 1)][4 * (g // 2) : P, cols], in_=y_grouped[item][:]
             )
             tokens = slice(c * CHUNK + h * HALF, c * CHUNK + (h + 1) * HALF)
             nc.sync.dma_start(
                 out=out_1[g, :, tokens, :].rearrange("p m t -> p (m t)").bitcast(I32), in_=codes[:].bitcast(I32)
             )
-            if (g, h) == (N // PASS - 1, 1):
+            if g != 1 and h == 1:
+                groups = slice(0, 1) if g == 0 else slice(1, 3)
+                rows = 4 * (groups.stop - groups.start)
                 for q in range(4):
-                    nc.sync.dma_start(
-                        out=out_2[:, 4 * q : 4 * q + 4, c * CHUNK : (c + 1) * CHUNK].bitcast(I32),
-                        in_=y_planes[c][32 * q : 32 * q + 12, :].bitcast(I32),
+                    queue = nc.scalar if item == order[-1] and q % 2 == 1 else nc.sync
+                    queue.dma_start(
+                        out=out_2[groups, 4 * q : 4 * q + 4, c * CHUNK : (c + 1) * CHUNK].bitcast(I32),
+                        in_=y_planes[c, min(g, 1)][32 * q : 32 * q + rows, :].bitcast(I32),
                     )
 
         order = step_order()
@@ -334,14 +341,11 @@ def tile_fourier_sine_field_planes_h1_kernel(
                 if on_scalar(n):
                     count_on_scalar(item)
             for item in at(n - 5, "second"):
-                if steps - TAIL <= n - 5 < steps - LAST:
-                    round_y(item, nc.scalar.copy)
                 turn_y(item)
             for c, h in x_for(n + 3):
                 turn_x(c, h, nc.vector.tensor_copy if c < XV else nc.scalar.copy)
             for item in at(n - 4, "second"):
-                if not steps - TAIL <= n - 4 < steps - LAST:
-                    round_y(item, nc.vector.tensor_copy)
+                round_y(item, nc.scalar.copy if steps - TAIL <= n - 4 < steps - LAST else nc.vector.tensor_copy)
             for item in at(n - DA - 1, "first"):
                 quantize_h(item)
             for c, h in x_for(n + 2):

import math
from contextlib import ExitStack

import concourse.mybir as mybir
from concourse.masks import make_identity

M, K, F, N = 2048, 512, 1024, 1536
FLOPS = 2 * M * K * F + 2 * M * F * N

F32 = mybir.dt.float32
BF16 = mybir.dt.bfloat16
I32 = mybir.dt.int32
U32 = mybir.dt.uint32
U8 = mybir.dt.uint8
FP8X4 = mybir.dt.float8_e4m3fn_x4
FP4X4 = mybir.dt.float4_e2m1fn_x4
ALU = mybir.AluOpType
ACT = mybir.ActivationFunctionType

P = 128
PASS = 512
CHUNK = 512
HALF = 256
CHUNKS = M // CHUNK
TURN = 2.0 * math.pi
ROUNDER = 1.5 * 2.0**23
SCALAR_ROUNDS_EVERY = 8
TAIL = 4
SHARED = 1
LAST = 2
FROM = 0
HEAD = 8
XV = 1
PH = 6
DA = 3


def step_order():
    first = [("first", c, g, h) for c in range(CHUNKS) for h in range(2) for g in range(F // PASS)]
    second = [("second", c, g, h) for c in range(CHUNKS) for g in range(N // PASS) for h in range(2)]
    order = first[:HEAD]
    for i in range(HEAD, len(first), 2):
        order = order + second[i - HEAD : i - HEAD + 2] + first[i : i + 2]
    return order + second[len(first) - HEAD :]


def tile_fourier_sine_field_planes_h1_kernel(
    tc, x, w1_words, w1_scales, a1, w2_words, w2_scales, b2, a2, out_0, out_1, out_2
):
    nc = tc.nc
    with ExitStack() as ctx:
        keep = ctx.enter_context(tc.tile_pool(name="keep", bufs=1))
        work = ctx.enter_context(tc.tile_pool(name="work", bufs=3))
        psum = ctx.enter_context(tc.psum_pool(name="psum", bufs=8))
        ctx.enter_context(tc.manual_schedule())

        def bank(shape):
            return psum.tile(shape, F32, name="bank")

        ident = keep.tile([P, P], F32, name="ident")
        make_identity(nc, ident[:])
        w1_plane = keep.tile([P, F], U8, name="w1_plane", align_bytes=64)
        nc.vector.memset(w1_plane[:].bitcast(I32), 0)
        b2_rows = keep.tile([P, P], BF16, name="b2_rows")
        nc.vector.memset(b2_rows[:], 0.0)
        w2_plane = keep.tile([P, 2, N], U8, name="w2_plane", align_bytes=64)
        nc.gpsimd.memset(w2_plane[:].rearrange("p g n -> p (g n)").bitcast(I32), 0)
        warm_in = keep.tile([P, 1], F32, name="warm_in")
        nc.vector.memset(warm_in[:], 0.0)
        warm_out = keep.tile([P, 1], F32, name="warm_out")
        nc.scalar.activation(out=warm_out[:], in_=warm_in[:], func=ACT.Sin)

        x_in = {}

        def load_x(c, h):
            x_half = keep.tile([P, 2, K], BF16, name="x_%d_%d" % (c, h))
            rows = x[c * CHUNK + h * HALF : c * CHUNK + (h + 1) * HALF, :]
            nc.sync.dma_start(out=x_half[:], in_=rows.rearrange("(j p) k -> p j k", p=P))
            x_in[c, h] = x_half

        load_x(0, 0)
        w1 = keep.tile([P, 2 * F], U8, name="w1", align_bytes=64)
        nc.sync.dma_start(out=w1[:].bitcast(I32), in_=w1_words[0].bitcast(I32))
        for q in range(4):
            nc.sync.dma_start(
                out=w1_plane[32 * q : 32 * q + 4, :].bitcast(I32),
                in_=w1_scales[0, 4 * q : 4 * q + 4, :].bitcast(I32),
            )
        load_x(0, 1)
        a1_sb = keep.tile([P, F // PASS, 4], BF16, name="a1_sb")
        nc.sync.dma_start(out=a1_sb[:], in_=a1.rearrange("(g p t) -> p g t", p=P, t=4))
        load_x(1, 0)
        load_x(1, 1)
        nc.sync.dma_start(out=b2_rows[0 : N // P, :], in_=b2.rearrange("(f p) -> f p", p=P))
        w2 = keep.tile([P, 2, 2 * N], U8, name="w2", align_bytes=64)
        nc.sync.dma_start(out=w2[:].bitcast(I32), in_=w2_words.rearrange("g p b -> p g b").bitcast(I32))
        for q in range(4):
            nc.sync.dma_start(
                out=w2_plane[32 * q : 32 * q + 4, :, :].bitcast(I32),
                in_=w2_scales[:, 4 * q : 4 * q + 4, :].rearrange("g r n -> r g n").bitcast(I32),
            )
        a2_sb = keep.tile([P, N], BF16, name="a2_sb")
        nc.sync.dma_start(out=a2_sb[:], in_=a2.partition_broadcast(P))
        for c in range(2, CHUNKS):
            for h in range(2):
                load_x(c, h)

        b2_turns = keep.tile([P, N // P], F32, name="b2_turns")

        b2_wide = keep.tile([P, P], F32, name="b2_wide")

        def scale_b2():
            nc.vector.tensor_scalar(out=b2_wide[:], in0=b2_rows[:], scalar1=1.0 / TURN, scalar2=None, op0=ALU.mult)

        def spread_b2():
            turned = bank([P, P])
            nc.tensor.transpose(turned[:], b2_wide[:], ident[:])
            nc.scalar.copy(out=b2_turns[:], in_=turned[:, 0 : N // P])

        def turn_words(word_blocks, name, copy):
            turned = bank([P, 2, 2, P])
            for j in range(2):
                for u in range(2):
                    nc.tensor.transpose(turned[:, j, u, :], word_blocks(j, u), ident[:])
            grouped = work.tile([P, 4 * HALF], BF16, name=name, align_bytes=64)
            copy(
                out=grouped[:].bitcast(F32).rearrange("p (j r u) -> p j r u", j=2, u=2),
                in_=turned[:].rearrange("p j u r -> p j r u"),
            )
            return grouped

        x_grouped, x_q = {}, {}

        def turn_x(c, h, copy):
            words = x_in[c, h][:].rearrange("p j k -> p (j k)").bitcast(F32)
            x_grouped[c, h] = turn_words(lambda j, u: words[:, 256 * j + u : 256 * (j + 1) : 2], "x_grouped", copy)

        def quantize_x(c, h):
            codes = work.tile([P, HALF], U32, name="x_codes", align_bytes=64)
            plane = work.tile([P, HALF], U8, name="x_plane", align_bytes=64)
            nc.vector.quantize_mx(out=codes[:].bitcast(FP8X4), scales=plane[:], in_=x_grouped[c, h][:])
            x_q[c, h] = (codes, plane)

        h_q = {}
        for c in range(CHUNKS):
            for g in range(F // PASS):
                h_codes = keep.tile([P, CHUNK], U32, name="h_codes_%d_%d" % (c, g), align_bytes=64)
                h_plane = keep.tile([P, CHUNK], U8, name="h_plane_%d_%d" % (c, g), align_bytes=64)
                h_q[c, g] = (h_codes, h_plane)
        y_planes = {}
        for c in range(CHUNKS):
            for pair in range(2):
                y_plane = keep.tile([P, CHUNK], U8, name="y_plane_%d_%d" % (c, pair), align_bytes=64)
                y_planes[c, pair] = y_plane

        turns, counts, rest, sines, rounded, results, y_grouped = {}, {}, {}, {}, {}, {}, {}

        def multiply(item):
            kind, c, g, h = item
            angle = work.tile([P, 2, PASS], F32, name="angle", bufs=6)
            for j in range(2):
                if kind == "first":
                    z = bank([P, PASS])
                    codes, plane = x_q[c, h]
                    nc.tensor.matmul_mx(
                        out=z[:],
                        lhsT=codes[:, P * j : P * (j + 1)].bitcast(FP8X4),
                        lhsT_scale=plane[:, P * j : P * (j + 1)],
                        rhs=w1[:, 2 * PASS * g : 2 * PASS * (g + 1)].bitcast(FP4X4),
                        rhs_scale=w1_plane[:, PASS * g : PASS * (g + 1)],
                        start=True,
                        stop=True,
                    )
                    sorted_out = angle[:, j, :].rearrange("p (t m) -> p t m", t=4)
                    sorted_in = z[:].rearrange("p (m t) -> p t m", t=4)
                    if j == 1 and item in order[:SHARED]:
                        nc.vector.tensor_scalar(
                            out=sorted_out, in0=sorted_in, scalar1=1.0 / TURN, scalar2=None, op0=ALU.mult
                        )
                    else:
                        nc.scalar.activation(out=sorted_out, in_=sorted_in, func=ACT.Copy, scale=1.0 / TURN)
                else:
                    z = bank([P, CHUNK])
                    block = 4 * g + 2 * h + j
                    for k in range(F // PASS):
                        nc.tensor.matmul_mx(
                            out=z[:],
                            lhsT=w2[:, k, 2 * P * block : 2 * P * (block + 1)].bitcast(FP4X4),
                            lhsT_scale=w2_plane[:, k, P * block : P * (block + 1)],
                            rhs=h_q[c, k][0][:].bitcast(FP8X4),
                            rhs_scale=h_q[c, k][1][:],
                            start=(k == 0),
                            stop=(k == F // PASS - 1),
                        )
                    nc.scalar.activation(
                        out=angle[:, j, :],
                        in_=z[:],
                        func=ACT.Identity,
                        scale=1.0 / TURN,
                        bias=b2_turns[:, block : block + 1],
                    )
            turns[item] = angle

        def count_on_scalar(item):
            count = work.tile([P, 2, PASS], U32, name="count")
            nc.scalar.activation(out=count[:], in_=turns[item][:], func=ACT.Copy, bias=ROUNDER)
            counts[item] = count[:].bitcast(I32)

        def count_on_vector(item):
            count = work.tile([P, 2, PASS], I32, name="count")
            nc.vector.tensor_scalar(out=count[:], in0=turns[item][:], scalar1=ROUNDER, scalar2=None, op0=ALU.add)
            counts[item] = count[:]

        def reduce_angle(item):
            part = work.tile([P, 2, PASS], F32, name="part", bufs=5)
            nc.vector.tensor_scalar(
                out=part[:], in0=counts[item], scalar1=ROUNDER, scalar2=-1.0, op0=ALU.subtract, op1=ALU.mult
            )
            rest[item] = part

        def sine(item):
            kind, c, g, h = item
            s = work.tile([P, 2, PASS], F32, name="sine")
            for j in range(2):
                frac = bank([P, 4, P])
                for b in range(4):
                    if kind == "first":
                        source, row, cols = item, j, slice(b * P, (b + 1) * P)
                    else:
                        source, row, cols = (kind, c, g, b // 2), b % 2, slice((2 * h + j) * P, (2 * h + j + 1) * P)
                    nc.tensor.matmul(
                        frac[:, b, :], lhsT=rest[source][:, row, cols], rhs=ident[:],
                        is_transpose=True, start=True, stop=False,
                    )
                    nc.tensor.matmul(
                        frac[:, b, :], lhsT=turns[source][:, row, cols], rhs=ident[:],
                        is_transpose=True, start=False, stop=True,
                    )
                if kind == "first":
                    nc.scalar.activation(
                        out=s[:, j, :].rearrange("p (n t) -> p n t", t=4),
                        in_=frac[:].rearrange("p t n -> p n t"), func=ACT.Sin, scale=TURN
                    )
                else:
                    nc.scalar.activation(
                        out=s[:, j, :], in_=frac[:].rearrange("p b f -> p (b f)"), func=ACT.Sin, scale=TURN
                    )
            sines[item] = s

        def amplify(item):
            kind, c, g, h = item
            if kind == "first":
                hb = work.tile([P, 4 * HALF], BF16, name="h_grouped", align_bytes=64)
                nc.vector.tensor_tensor(
                    out=hb[:].rearrange("p (n t) -> p n t", t=4),
                    in0=sines[item][:].rearrange("p j (n t) -> p (j n) t", t=4),
                    in1=a1_sb[:, g, :].unsqueeze(1).to_broadcast([P, HALF, 4]),
                    op=ALU.mult,
                )
                rounded[item] = hb
            else:
                y = work.tile([P, 2, PASS], F32, name="y", bufs=4)
                nc.vector.tensor_tensor(
                    out=y[:],
                    in0=sines[item][:],
                    in1=a2_sb[:, g * PASS : (g + 1) * PASS].unsqueeze(1).to_broadcast([P, 2, PASS]),
                    op=ALU.mult,
                )
                rows = out_0[c * CHUNK + h * HALF : c * CHUNK + (h + 1) * HALF, g * PASS : (g + 1) * PASS]
                nc.sync.dma_start(out=rows.rearrange("(j p) n -> p j n", p=P), in_=y[:])
                results[item] = y

        def round_y(item, copy):
            yb = work.tile([P, 2, 2, P, 2], BF16, name="y_sorted")
            copy(out=yb[:], in_=results[item][:].rearrange("p j (m u e) -> p j u m e", u=2, e=2))
            rounded[item] = yb

        def turn_y(item):
            words = rounded[item][:].rearrange("p j u m e -> p (j u m e)").bitcast(F32)
            y_grouped[item] = turn_words(lambda j, u: words[:, (2 * j + u) * P : (2 * j + u + 1) * P], "y_grouped", nc.scalar.copy)

        def quantize_h(item):
            kind, c, g, h = item
            cols = slice(h * HALF, (h + 1) * HALF)
            nc.vector.quantize_mx(
                out=h_q[c, g][0][:, cols].bitcast(FP8X4), scales=h_q[c, g][1][:, cols], in_=rounded[item][:]
            )

        def quantize_y(item):
            kind, c, g, h = item
            cols = slice(h * HALF, (h + 1) * HALF)
            codes = work.tile([P, HALF], U32, name="y_codes", align_bytes=64)
            nc.vector.quantize_mx(
                out=codes[:].bitcast(FP8X4), scales=y_planes[c, min(g, 1)][4 * (g // 2) : P, cols], in_=y_grouped[item][:]
            )
            tokens = slice(c * CHUNK + h * HALF, c * CHUNK + (h + 1) * HALF)
            nc.sync.dma_start(
                out=out_1[g, :, tokens, :].rearrange("p m t -> p (m t)").bitcast(I32), in_=codes[:].bitcast(I32)
            )
            if g != 1 and h == 1:
                groups = slice(0, 1) if g == 0 else slice(1, 3)
                rows = 4 * (groups.stop - groups.start)
                for q in range(4):
                    queue = nc.scalar if item == order[-1] and q % 2 == 1 else nc.sync
                    queue.dma_start(
                        out=out_2[groups, 4 * q : 4 * q + 4, c * CHUNK : (c + 1) * CHUNK].bitcast(I32),
                        in_=y_planes[c, min(g, 1)][32 * q : 32 * q + rows, :].bitcast(I32),
                    )

        order = step_order()

        def at(n, kind=None):
            if 0 <= n < len(order) and kind in (None, order[n][0]):
                return [order[n]]
            return []

        def x_for(n):
            return [(c, h) for (kind, c, g, h) in at(n, "first") if g == 0]

        turn_x(0, 0, nc.vector.tensor_copy)
        quantize_x(0, 0)
        turn_x(0, 1, nc.vector.tensor_copy)
        steps = len(order)

        def on_scalar(i):
            return i % SCALAR_ROUNDS_EVERY == PH and i >= FROM

        for n in range(steps + 7):
            for item in at(n):
                multiply(item)
            for item in at(n - 1):
                if not on_scalar(n - 1):
                    count_on_vector(item)
            for item in at(n - DA, "first") + at(n - 3, "second"):
                sine(item)
            for item in at(n - DA - 1, "first") + at(n - 4, "second"):
                amplify(item)
            for item in at(n - 1):
                reduce_angle(item)
            for item in at(n):
                if on_scalar(n):
                    count_on_scalar(item)
            for item in at(n - 5, "second"):
                turn_y(item)
            for c, h in x_for(n + 3):
                turn_x(c, h, nc.vector.tensor_copy if c < XV else nc.scalar.copy)
            for item in at(n - 4, "second"):
                round_y(item, nc.scalar.copy if steps - TAIL <= n - 4 < steps - LAST else nc.vector.tensor_copy)
            for item in at(n - DA - 1, "first"):
                quantize_h(item)
            for c, h in x_for(n + 2):
                quantize_x(c, h)
            for item in at(n - 6, "second"):
                quantize_y(item)
            if n == 2:
                scale_b2()
            if n == 4:
                spread_b2()
